import numpy as np
import ml_dtypes


def mxq(x, axis, fmt="e4m3"):
    dtype, down = {"e4m3": (ml_dtypes.float8_e4m3fn, 7), "e5m2": (ml_dtypes.float8_e5m2, 14)}[fmt]
    v = np.moveaxis(np.asarray(x, np.float32).astype(ml_dtypes.bfloat16).astype(np.float64), axis, -1)
    blocks = v.reshape(v.shape[:-1] + (-1, 32))
    amax = np.abs(blocks).max(-1, keepdims=True)
    byte = np.maximum(np.where(amax > 0, np.frexp(amax)[1] - 1 + 127, 0) - down, 1)
    scale = np.exp2(byte - 127.0)
    codes = (blocks / scale).astype(np.float32).astype(dtype).astype(np.float64)
    return np.moveaxis((codes * scale).reshape(v.shape), -1, axis)


WIDE = False


def mx_kscale(k):
    if not WIDE:
        return np.ones(k)
    levels = np.array([10, -10, 5, -5, 0])
    if k % 512:
        return np.exp2(np.random.permutation(np.resize(levels, k // 32))).repeat(32)
    a = np.empty((k // 512, 16))
    for p in range(k // 512):
        a[p, :8] = np.random.permutation(np.resize(levels, 8))
        for g in range(8):
            far = levels[np.abs(levels - a[p, g]) >= 10]
            a[p, g + 8] = far[np.random.randint(len(far))]
    return np.exp2(a.ravel()).repeat(32)


def f64(x):
    return np.asarray(x).astype(np.float64)


def striped(idx):
    return np.tile(idx.reshape(-1, 16).T, (8, 1)).astype(np.uint16)


def unstriped(offs):
    return offs[:16].T.reshape(-1).astype(np.int64)


E2M1 = np.array([0.0, 0.5, 1.0, 1.5, 2.0, 3.0, 4.0, 6.0, -0.0, -0.5, -1.0, -1.5, -2.0, -3.0, -4.0, -6.0])


def pack_fp4(w):
    k, n = w.shape
    w = f64(np.asarray(w, np.float32).astype(ml_dtypes.bfloat16)).reshape(k // 32, 32, n)
    amax = np.abs(w).max(1)
    mant, ex = np.frexp(amax / 6.0)
    byte = np.clip(np.where(amax > 0, np.where(mant > 0.5, ex, ex - 1) + 127, 1), 1, 254)
    scaled = (w * np.exp2(127.0 - byte)[:, None, :]).reshape(k, n).astype(np.float32)
    c = np.ascontiguousarray(scaled.reshape(k // 512, 128, 4, n).transpose(0, 1, 3, 2)).astype(ml_dtypes.float4_e2m1fn).view(np.uint8) & 0xF
    words = (c[..., 0::2] | (c[..., 1::2] << 4)).reshape(k // 512, 128, 2 * n)
    return np.ascontiguousarray(words), np.ascontiguousarray(byte.astype(np.uint8).reshape(k // 512, 16, n))


def unpack_fp4(words, scales):
    g, _, n = scales.shape
    words = np.ascontiguousarray(words).reshape(g, 128, n, 2)
    nib = np.empty((g, 128, n, 4), np.uint8)
    nib[..., 0::2] = words & 0xF
    nib[..., 1::2] = words >> 4
    vals = E2M1[nib] * np.repeat(np.exp2(scales.astype(np.float64) - 127.0), 8, axis=1)[..., None]
    return vals.transpose(0, 1, 3, 2).reshape(g * 512, n)


def relu(v):
    return np.maximum(v, 0.0)


K, T, S, V, N, U = 1024, 2048, 1536, 512, 128, 1024


def setup_inputs():
    n = np.random.standard_normal
    s = mx_kscale(K)[:, None]
    packed_w1 = pack_fp4(n((K, N)) / np.sqrt(3 * K) / s)
    packed_w2 = pack_fp4(n((K, N)) / np.sqrt(3 * K) / s)
    packed_w3 = pack_fp4(n((K, N)) / np.sqrt(3 * K) / s)
    return {
        "xT": (n((K, T)) * s).astype(np.float32),
        "w1_words": packed_w1[0],
        "w1_scales": packed_w1[1],
        "w2_words": packed_w2[0],
        "w2_scales": packed_w2[1],
        "w3_words": packed_w3[0],
        "w3_scales": packed_w3[1],
        "offs": striped(np.random.permutation(T)[:S]),
        "to1": striped(np.random.permutation(U)[:V]),
        "to2": striped(np.random.permutation(U)[:V]),
        "to3": striped(np.random.permutation(U)[:V]),
    }


def reference(xT, w1_words, w1_scales, w2_words, w2_scales, w3_words, w3_scales, offs, to1, to2, to3):
    xq = mxq(f64(xT)[:, unstriped(offs)], 0, "e4m3")
    o0 = np.zeros((N, U))
    o0[:, unstriped(to1)] = unpack_fp4(w1_words, w1_scales).T @ xq[:, :V]
    o1 = np.zeros((N, U))
    o1[:, unstriped(to2)] = unpack_fp4(w2_words, w2_scales).T @ xq[:, V:2 * V]
    o2 = np.zeros((N, U))
    o2[:, unstriped(to3)] = unpack_fp4(w3_words, w3_scales).T @ xq[:, 2 * V:3 * V]
    return relu(o0 + o1 + o2)

@@ -1,0 +1,190 @@
+from contextlib import ExitStack
+
+import concourse.mybir as mybir
+from concourse.masks import make_identity
+
+K, T, S, V, N, U = 1024, 2048, 1536, 512, 128, 1024
+TAPS = 3
+FLOPS = 2 * K * S * N
+
+F32 = mybir.dt.float32
+BF16 = mybir.dt.bfloat16
+I32 = mybir.dt.int32
+U32 = mybir.dt.uint32
+U16 = mybir.dt.uint16
+U8 = mybir.dt.uint8
+FP8X4 = mybir.dt.float8_e4m3fn_x4
+FP4X4 = mybir.dt.float4_e2m1fn_x4
+ADD = mybir.AluOpType.add
+RELU = mybir.ActivationFunctionType.Relu
+
+P = 128
+PASSES = K // (4 * P)
+LIST_COLS = V // 16
+BANK = 512
+
+LOADS = (
+    ((0, 1024, 704), (1024, 2048, 704)),
+    ((0, 1024, 0), (1024, 2048, 704)),
+    ((0, 1024, 0), (1024, 2048, 0)),
+    ((0, 1024, 0), (1024, 1536, 0), (1536, 2048, 0)),
+)
+OUT_CHUNK = 256
+
+
+def tile_picked_spconv_relu_e_kernel(
+    tc, xT, w1_words, w1_scales, w2_words, w2_scales, w3_words, w3_scales, offs, to1, to2, to3, out
+):
+    nc = tc.nc
+    with ExitStack() as ctx:
+        keep = ctx.enter_context(tc.tile_pool(name="keep", bufs=1))
+        psum = ctx.enter_context(tc.psum_pool(name="psum", bufs=1))
+
+        picks = keep.tile([P, S // 16], U16, name="picks")
+        nc.sync.dma_start(picks[:], offs)
+
+        x_rows = xT.rearrange("(g p u e) t -> g u p e t", g=PASSES, p=P, u=2, e=2)
+        raw = {}
+        for q in range(2 * PASSES):
+            for i, (c0, c1, on_vector) in enumerate(LOADS[q]):
+                raw[q, i] = keep.tile([P, 2, c1 - c0], F32, name=f"raw{q}_{i}", tag=f"raw{q}_{i}", align_bytes=64)
+                nc.sync.dma_start(raw[q, i][:], x_rows[q // 2, q % 2, :, :, c0:c1])
+
+        w_codes = []
+        for d, words in enumerate((w1_words, w2_words, w3_words)):
+            w_codes.append(keep.tile([P, PASSES, 2 * N], U8, name=f"w_codes{d}", align_bytes=64))
+            nc.sync.dma_start(w_codes[d][:].bitcast(I32), words.bitcast(I32).rearrange("g p n -> p g n"))
+        places = []
+        for d, to in enumerate((to1, to2, to3)):
+            places.append(keep.tile([P, LIST_COLS], U16, name=f"places{d}"))
+            nc.sync.dma_start(places[d][:], to)
+
+        w_scales = keep.tile([P, TAPS * PASSES, N], U8, name="w_scales", align_bytes=64)
+        nc.vector.memset(w_scales[:].bitcast(I32), 0)
+        for d, scales in enumerate((w1_scales, w2_scales, w3_scales)):
+            for quad in range(4):
+                nc.gpsimd.dma_start(
+                    w_scales[32 * quad : 32 * quad + 4, PASSES * d : PASSES * (d + 1), :].bitcast(I32),
+                    scales.bitcast(I32)[:, 4 * quad : 4 * quad + 4, :].rearrange("g j n -> j g n"),
+                )
+
+        spread = []
+        for d in range(TAPS):
+            spread.append(keep.tile([P, U], F32, name=f"spread{d}"))
+            nc.vector.memset(spread[d][:], 0.0)
+        ident = keep.tile([P, P], F32, name="ident")
+        make_identity(nc, ident[:])
+
+        pairs = [keep.tile([P, 2 * T], BF16, name=f"pairs{q}") for q in range(2 * PASSES)]
+        picked = [keep.tile([P, 2, S], U32, name=f"picked{g}") for g in range(PASSES)]
+        acc = [psum.tile([P, V], F32, name=f"acc{d}") for d in range(TAPS)]
+        woven = {}
+        codes = {}
+        scale = {}
+
+        def cast(q):
+            dst = pairs[q][:].rearrange("p (t e) -> p t e", e=2)
+            for i, (c0, c1, on_vector) in enumerate(LOADS[q]):
+                src = raw[q, i][:].rearrange("p e t -> p t e")
+                if on_vector:
+                    nc.vector.tensor_copy(dst[:, c0 : c0 + on_vector, :], src[:, :on_vector, :])
+                nc.scalar.copy(dst[:, c0 + on_vector : c1, :], src[:, on_vector:, :])
+
+        def gather(q, first, last):
+            window = pairs[q][:].bitcast(U32)
+            nc.vector.tensor_copy(
+                picked[q // 2][:, q % 2, V * first : V * last],
+                window.indirect(picks[:, LIST_COLS * first : LIST_COLS * last]),
+            )
+
+        def weave(g, d, on_vector, tag):
+            woven[g, d] = keep.tile([P, 4 * V], BF16, name=f"woven{g}_{d}", tag=tag, align_bytes=64)
+            src = picked[g][:, :, V * d : V * (d + 1)]
+            if on_vector:
+                nc.vector.tensor_copy(
+                    woven[g, d][:].bitcast(I32).rearrange("p (v u) -> p v u", u=2),
+                    src.bitcast(I32).rearrange("p u v -> p v u"),
+                )
+            else:
+                nc.scalar.copy(
+                    woven[g, d][:].bitcast(U32).rearrange("p (v u) -> p v u", u=2),
+                    src.rearrange("p u v -> p v u"),
+                )
+
+        def quantise(g, d):
+            codes[g, d] = keep.tile([P, V], U32, name=f"codes{g}_{d}", align_bytes=64)
+            scale[g, d] = keep.tile([P, V], U8, name=f"scale{g}_{d}", align_bytes=64)
+            nc.vector.quantize_mx(out=codes[g, d][:].bitcast(FP8X4), scales=scale[g, d][:], in_=woven[g, d][:])
+
+        def multiply(g, d):
+            nc.tensor.matmul_mx(
+                out=acc[d][:],
+                lhsT=w_codes[d][:, g, :].bitcast(FP4X4),
+                lhsT_scale=w_scales[:, PASSES * d + g, :],
+                rhs=codes[g, d][:].bitcast(FP8X4),
+                rhs_scale=scale[g, d][:],
+                start=(g == 0),
+                stop=(g == PASSES - 1),
+            )
+
+        cast(0)
+        gather(0, 0, TAPS)
+        cast(1)
+        for d in range(TAPS):
+            gather(1, d, d + 1)
+        cast(2)
+        weave(0, 0, True, "woven0_0")
+        weave(0, 1, True, "woven0_1")
+        quantise(0, 0)
+        quantise(0, 1)
+        gather(2, 0, TAPS)
+        cast(3)
+        weave(0, 2, False, "raw3_2")
+        for d in range(TAPS):
+            gather(3, d, d + 1)
+        for d in range(TAPS):
+            weave(1, d, False, f"woven1_{d}")
+        multiply(0, 0)
+        multiply(0, 1)
+        quantise(1, 0)
+        quantise(0, 2)
+        quantise(1, 1)
+        quantise(1, 2)
+        multiply(1, 0)
+        multiply(1, 1)
+        multiply(0, 2)
+        multiply(1, 2)
+
+        for d in range(TAPS):
+            y = keep.tile([P, V], F32, name=f"y{d}")
+            nc.scalar.copy(y[:], acc[d][:])
+            nc.vector.tensor_copy(spread[d][:].indirect(places[d][:]), y[:])
+
+        halves = U // BANK
+        blocks = BANK // P
+        turned = [psum.tile([P, BANK], F32, name=f"turned{h}") for h in range(halves)]
+        for d in range(2):
+            for h in range(halves):
+                for b in range(blocks):
+                    nc.tensor.matmul(
+                        turned[h][:, P * b : P * (b + 1)],
+                        spread[d][:, BANK * h + P * b : BANK * h + P * (b + 1)],
+                        ident[:],
+                        start=(d == 0 and b == 0),
+                        stop=(d == 1 and b == blocks - 1),
+                        is_transpose=True,
+                    )
+        two_taps = [psum.tile([P, BANK], F32, name=f"two_taps{h}") for h in range(halves)]
+        for h in range(halves):
+            held = keep.tile([P, BANK], F32, name=f"held{h}")
+            nc.scalar.copy(held[:], turned[h][:])
+            for b in range(blocks):
+                nc.tensor.transpose(two_taps[h][:, P * b : P * (b + 1)], held[:, P * b : P * (b + 1)], ident[:])
+
+        for c0 in range(0, U, OUT_CHUNK):
+            h, at = divmod(c0, BANK)
+            total = keep.tile([P, OUT_CHUNK], F32, name=f"total{c0}")
+            result = keep.tile([P, OUT_CHUNK], F32, name=f"result{c0}")
+            nc.vector.tensor_tensor(total[:], spread[2][:, c0 : c0 + OUT_CHUNK], two_taps[h][:, at : at + OUT_CHUNK], ADD)
+            nc.scalar.activation(result[:], total[:], RELU)
+            nc.sync.dma_start(out[:, c0 : c0 + OUT_CHUNK], result[:])

@@ -27,7 +27,7 @@ LOADS = (
     ((0, 1024, 704), (1024, 2048, 704)),
     ((0, 1024, 0), (1024, 2048, 704)),
     ((0, 1024, 0), (1024, 2048, 0)),
-    ((0, 1024, 0), (1024, 1536, 0), (1536, 2048, 0)),
+    ((0, 1024, 0), (1024, 1536, 0), (1536, 2048, 192)),
 )
 OUT_CHUNK = 256
 
@@ -40,15 +40,29 @@ def tile_picked_spconv_relu_e_kernel(
         keep = ctx.enter_context(tc.tile_pool(name="keep", bufs=1))
         psum = ctx.enter_context(tc.psum_pool(name="psum", bufs=1))
 
-        picks = keep.tile([P, S // 16], U16, name="picks")
-        nc.sync.dma_start(picks[:], offs)
+        w_scales = keep.tile([P, TAPS * PASSES, N], U8, name="w_scales", align_bytes=64)
+        nc.gpsimd.memset(w_scales[:].bitcast(I32), 0)
+        scale_loads = [
+            (
+                w_scales[32 * quad : 32 * quad + 4, PASSES * d : PASSES * (d + 1), :].bitcast(I32),
+                scales.bitcast(I32)[:, 4 * quad : 4 * quad + 4, :].rearrange("g j n -> j g n"),
+            )
+            for d, scales in enumerate((w1_scales, w2_scales, w3_scales))
+            for quad in range(4)
+        ]
 
+        picks = keep.tile([P, S // 16], U16, name="picks")
         x_rows = xT.rearrange("(g p u e) t -> g u p e t", g=PASSES, p=P, u=2, e=2)
         raw = {}
         for q in range(2 * PASSES):
             for i, (c0, c1, on_vector) in enumerate(LOADS[q]):
+                if len(raw) >= 3:
+                    for rows, source in scale_loads[2 * (len(raw) - 3) : 2 * (len(raw) - 2)]:
+                        nc.sync.dma_start(rows, source)
                 raw[q, i] = keep.tile([P, 2, c1 - c0], F32, name=f"raw{q}_{i}", tag=f"raw{q}_{i}", align_bytes=64)
                 nc.sync.dma_start(raw[q, i][:], x_rows[q // 2, q % 2, :, :, c0:c1])
+                if len(raw) == 1:
+                    nc.sync.dma_start(picks[:], offs)
 
         w_codes = []
         for d, words in enumerate((w1_words, w2_words, w3_words)):
@@ -58,15 +72,6 @@ def tile_picked_spconv_relu_e_kernel(
         for d, to in enumerate((to1, to2, to3)):
             places.append(keep.tile([P, LIST_COLS], U16, name=f"places{d}"))
             nc.sync.dma_start(places[d][:], to)
-
-        w_scales = keep.tile([P, TAPS * PASSES, N], U8, name="w_scales", align_bytes=64)
-        nc.vector.memset(w_scales[:].bitcast(I32), 0)
-        for d, scales in enumerate((w1_scales, w2_scales, w3_scales)):
-            for quad in range(4):
-                nc.gpsimd.dma_start(
-                    w_scales[32 * quad : 32 * quad + 4, PASSES * d : PASSES * (d + 1), :].bitcast(I32),
-                    scales.bitcast(I32)[:, 4 * quad : 4 * quad + 4, :].rearrange("g j n -> j g n"),
-                )
 
         spread = []
         for d in range(TAPS):
@@ -111,8 +116,8 @@ def tile_picked_spconv_relu_e_kernel(
                     src.rearrange("p u v -> p v u"),
                 )
 
-        def quantise(g, d):
-            codes[g, d] = keep.tile([P, V], U32, name=f"codes{g}_{d}", align_bytes=64)
+        def quantise(g, d, tag):
+            codes[g, d] = keep.tile([P, V], U32, name=f"codes{g}_{d}", tag=tag, align_bytes=64)
             scale[g, d] = keep.tile([P, V], U8, name=f"scale{g}_{d}", align_bytes=64)
             nc.vector.quantize_mx(out=codes[g, d][:].bitcast(FP8X4), scales=scale[g, d][:], in_=woven[g, d][:])
 
@@ -135,8 +140,8 @@ def tile_picked_spconv_relu_e_kernel(
         cast(2)
         weave(0, 0, True, "woven0_0")
         weave(0, 1, True, "woven0_1")
-        quantise(0, 0)
-        quantise(0, 1)
+        quantise(0, 0, "codes0_0")
+        quantise(0, 1, "codes0_1")
         gather(2, 0, TAPS)
         cast(3)
         weave(0, 2, False, "raw3_2")
@@ -146,10 +151,10 @@ def tile_picked_spconv_relu_e_kernel(
             weave(1, d, False, f"woven1_{d}")
         multiply(0, 0)
         multiply(0, 1)
-        quantise(1, 0)
-        quantise(0, 2)
-        quantise(1, 1)
-        quantise(1, 2)
+        quantise(1, 0, "codes1_0")
+        quantise(1, 1, "codes1_1")
+        quantise(0, 2, "woven1_1")
+        quantise(1, 2, "codes1_2")
         multiply(1, 0)
         multiply(1, 1)
         multiply(0, 2)

@@ -23,12 +23,8 @@ PASSES = K // (4 * P)
 LIST_COLS = V // 16
 BANK = 512
 
-LOADS = (
-    ((0, 1024, 704), (1024, 2048, 704)),
-    ((0, 1024, 0), (1024, 2048, 704)),
-    ((0, 1024, 0), (1024, 2048, 0)),
-    ((0, 1024, 0), (1024, 1536, 0), (1536, 2048, 192)),
-)
+SHARES = ((512, 512, 512, 352), (0, 0, 0, 416), (0, 0, 0, 0), (0, 0, 0, 256))
+LOADS = tuple(tuple((512 * i, 512 * (i + 1), share) for i, share in enumerate(shares)) for shares in SHARES)
 OUT_CHUNK = 256
 
 
@@ -56,8 +52,8 @@ def tile_picked_spconv_relu_e_kernel(
         raw = {}
         for q in range(2 * PASSES):
             for i, (c0, c1, on_vector) in enumerate(LOADS[q]):
-                if len(raw) >= 3:
-                    for rows, source in scale_loads[2 * (len(raw) - 3) : 2 * (len(raw) - 2)]:
+                if len(raw) >= 4:
+                    for rows, source in scale_loads[len(raw) - 4 : len(raw) - 3]:
                         nc.sync.dma_start(rows, source)
                 raw[q, i] = keep.tile([P, 2, c1 - c0], F32, name=f"raw{q}_{i}", tag=f"raw{q}_{i}", align_bytes=64)
                 nc.sync.dma_start(raw[q, i][:], x_rows[q // 2, q % 2, :, :, c0:c1])
@@ -83,7 +79,6 @@ def tile_picked_spconv_relu_e_kernel(
         pairs = [keep.tile([P, 2 * T], BF16, name=f"pairs{q}") for q in range(2 * PASSES)]
         picked = [keep.tile([P, 2, S], U32, name=f"picked{g}") for g in range(PASSES)]
         acc = [psum.tile([P, V], F32, name=f"acc{d}") for d in range(TAPS)]
-        woven = {}
         codes = {}
         scale = {}
 
@@ -93,7 +88,8 @@ def tile_picked_spconv_relu_e_kernel(
                 src = raw[q, i][:].rearrange("p e t -> p t e")
                 if on_vector:
                     nc.vector.tensor_copy(dst[:, c0 : c0 + on_vector, :], src[:, :on_vector, :])
-                nc.scalar.copy(dst[:, c0 + on_vector : c1, :], src[:, on_vector:, :])
+                if c0 + on_vector < c1:
+                    nc.scalar.copy(dst[:, c0 + on_vector : c1, :], src[:, on_vector:, :])
 
         def gather(q, first, last):
             window = pairs[q][:].bitcast(U32)
@@ -102,61 +98,70 @@ def tile_picked_spconv_relu_e_kernel(
                 window.indirect(picks[:, LIST_COLS * first : LIST_COLS * last]),
             )
 
-        def weave(g, d, on_vector, tag):
-            woven[g, d] = keep.tile([P, 4 * V], BF16, name=f"woven{g}_{d}", tag=tag, align_bytes=64)
+        def weave(g, d, into, on_vector):
             src = picked[g][:, :, V * d : V * (d + 1)]
             if on_vector:
                 nc.vector.tensor_copy(
-                    woven[g, d][:].bitcast(I32).rearrange("p (v u) -> p v u", u=2),
+                    into.bitcast(I32).rearrange("p (v u) -> p v u", u=2),
                     src.bitcast(I32).rearrange("p u v -> p v u"),
                 )
             else:
                 nc.scalar.copy(
-                    woven[g, d][:].bitcast(U32).rearrange("p (v u) -> p v u", u=2),
+                    into.bitcast(U32).rearrange("p (v u) -> p v u", u=2),
                     src.rearrange("p u v -> p v u"),
                 )
 
-        def quantise(g, d, tag):
-            codes[g, d] = keep.tile([P, V], U32, name=f"codes{g}_{d}", tag=tag, align_bytes=64)
-            scale[g, d] = keep.tile([P, V], U8, name=f"scale{g}_{d}", align_bytes=64)
-            nc.vector.quantize_mx(out=codes[g, d][:].bitcast(FP8X4), scales=scale[g, d][:], in_=woven[g, d][:])
+        def quantise(woven, operands, tag=None):
+            width = V * len(operands)
+            name = "_".join(f"{g}{d}" for g, d in operands)
+            words = keep.tile([P, width], U32, name=f"codes{name}", tag=tag or f"codes{name}", align_bytes=64)
+            planes = keep.tile([P, width], U8, name=f"scale{name}", align_bytes=64)
+            nc.vector.quantize_mx(out=words[:].bitcast(FP8X4), scales=planes[:], in_=woven[:])
+            for i, operand in enumerate(operands):
+                codes[operand] = words[:, V * i : V * (i + 1)]
+                scale[operand] = planes[:, V * i : V * (i + 1)]
 
         def multiply(g, d):
             nc.tensor.matmul_mx(
                 out=acc[d][:],
                 lhsT=w_codes[d][:, g, :].bitcast(FP4X4),
                 lhsT_scale=w_scales[:, PASSES * d + g, :],
-                rhs=codes[g, d][:].bitcast(FP8X4),
-                rhs_scale=scale[g, d][:],
+                rhs=codes[g, d].bitcast(FP8X4),
+                rhs_scale=scale[g, d],
                 start=(g == 0),
                 stop=(g == PASSES - 1),
             )
 
+        woven = {
+            (g, d): keep.tile([P, 4 * V], BF16, name=f"woven{g}_{d}", tag=f"woven{g}_{d}", align_bytes=64)
+            for g in range(PASSES)
+            for d in range(TAPS)
+            if (g, d) != (0, 2)
+        }
         cast(0)
         gather(0, 0, TAPS)
         cast(1)
-        for d in range(TAPS):
-            gather(1, d, d + 1)
+        gather(1, 0, 1)
+        gather(1, 1, TAPS)
         cast(2)
-        weave(0, 0, True, "woven0_0")
-        weave(0, 1, True, "woven0_1")
-        quantise(0, 0, "codes0_0")
-        quantise(0, 1, "codes0_1")
+        for d in range(2):
+            weave(0, d, woven[0, d][:], True)
+        for d in range(2):
+            quantise(woven[0, d], [(0, d)])
+            multiply(0, d)
         gather(2, 0, TAPS)
         cast(3)
-        weave(0, 2, False, "raw3_2")
+        woven[0, 2] = keep.tile([P, 4 * V], BF16, name="woven0_2", tag="raw3_3", align_bytes=64)
+        weave(0, 2, woven[0, 2][:], False)
         for d in range(TAPS):
             gather(3, d, d + 1)
         for d in range(TAPS):
-            weave(1, d, False, f"woven1_{d}")
-        multiply(0, 0)
-        multiply(0, 1)
-        quantise(1, 0, "codes1_0")
-        quantise(1, 1, "codes1_1")
-        quantise(0, 2, "woven1_1")
-        quantise(1, 2, "codes1_2")
-        multiply(1, 0)
-        multiply(1, 1)
+            weave(1, d, woven[1, d][:], False)
+        for d in range(2):
+            quantise(woven[1, d], [(1, d)])
+            multiply(1, d)
+        quantise(woven[0, 2], [(0, 2)], "woven1_1")
+        quantise(woven[1, 2], [(1, 2)])
         multiply(0, 2)
         multiply(1, 2)
 

from contextlib import ExitStack

import concourse.mybir as mybir
from concourse.masks import make_identity

K, T, S, V, N, U = 1024, 2048, 1536, 512, 128, 1024
TAPS = 3
FLOPS = 2 * K * S * N

F32 = mybir.dt.float32
BF16 = mybir.dt.bfloat16
I32 = mybir.dt.int32
U32 = mybir.dt.uint32
U16 = mybir.dt.uint16
U8 = mybir.dt.uint8
FP8X4 = mybir.dt.float8_e4m3fn_x4
FP4X4 = mybir.dt.float4_e2m1fn_x4
ADD = mybir.AluOpType.add
RELU = mybir.ActivationFunctionType.Relu

P = 128
PASSES = K // (4 * P)
LIST_COLS = V // 16
BANK = 512

SHARES = ((512, 512, 512, 352), (0, 0, 0, 416), (0, 0, 0, 0), (0, 0, 0, 256))
LOADS = tuple(tuple((512 * i, 512 * (i + 1), share) for i, share in enumerate(shares)) for shares in SHARES)
OUT_CHUNK = 256


def tile_picked_spconv_relu_e_kernel(
    tc, xT, w1_words, w1_scales, w2_words, w2_scales, w3_words, w3_scales, offs, to1, to2, to3, out
):
    nc = tc.nc
    with ExitStack() as ctx:
        keep = ctx.enter_context(tc.tile_pool(name="keep", bufs=1))
        psum = ctx.enter_context(tc.psum_pool(name="psum", bufs=1))

        w_scales = keep.tile([P, TAPS * PASSES, N], U8, name="w_scales", align_bytes=64)
        nc.gpsimd.memset(w_scales[:].bitcast(I32), 0)
        scale_loads = [
            (
                w_scales[32 * quad : 32 * quad + 4, PASSES * d : PASSES * (d + 1), :].bitcast(I32),
                scales.bitcast(I32)[:, 4 * quad : 4 * quad + 4, :].rearrange("g j n -> j g n"),
            )
            for d, scales in enumerate((w1_scales, w2_scales, w3_scales))
            for quad in range(4)
        ]

        picks = keep.tile([P, S // 16], U16, name="picks")
        x_rows = xT.rearrange("(g p u e) t -> g u p e t", g=PASSES, p=P, u=2, e=2)
        raw = {}
        for q in range(2 * PASSES):
            for i, (c0, c1, on_vector) in enumerate(LOADS[q]):
                if len(raw) >= 4:
                    for rows, source in scale_loads[len(raw) - 4 : len(raw) - 3]:
                        nc.sync.dma_start(rows, source)
                raw[q, i] = keep.tile([P, 2, c1 - c0], F32, name=f"raw{q}_{i}", tag=f"raw{q}_{i}", align_bytes=64)
                nc.sync.dma_start(raw[q, i][:], x_rows[q // 2, q % 2, :, :, c0:c1])
                if len(raw) == 1:
                    nc.sync.dma_start(picks[:], offs)

        w_codes = []
        for d, words in enumerate((w1_words, w2_words, w3_words)):
            w_codes.append(keep.tile([P, PASSES, 2 * N], U8, name=f"w_codes{d}", align_bytes=64))
            nc.sync.dma_start(w_codes[d][:].bitcast(I32), words.bitcast(I32).rearrange("g p n -> p g n"))
        places = []
        for d, to in enumerate((to1, to2, to3)):
            places.append(keep.tile([P, LIST_COLS], U16, name=f"places{d}"))
            nc.sync.dma_start(places[d][:], to)

        spread = []
        for d in range(TAPS):
            spread.append(keep.tile([P, U], F32, name=f"spread{d}"))
            nc.vector.memset(spread[d][:], 0.0)
        ident = keep.tile([P, P], F32, name="ident")
        make_identity(nc, ident[:])

        pairs = [keep.tile([P, 2 * T], BF16, name=f"pairs{q}") for q in range(2 * PASSES)]
        picked = [keep.tile([P, 2, S], U32, name=f"picked{g}") for g in range(PASSES)]
        acc = [psum.tile([P, V], F32, name=f"acc{d}") for d in range(TAPS)]
        codes = {}
        scale = {}

        def cast(q):
            dst = pairs[q][:].rearrange("p (t e) -> p t e", e=2)
            for i, (c0, c1, on_vector) in enumerate(LOADS[q]):
                src = raw[q, i][:].rearrange("p e t -> p t e")
                if on_vector:
                    nc.vector.tensor_copy(dst[:, c0 : c0 + on_vector, :], src[:, :on_vector, :])
                if c0 + on_vector < c1:
                    nc.scalar.copy(dst[:, c0 + on_vector : c1, :], src[:, on_vector:, :])

        def gather(q, first, last):
            window = pairs[q][:].bitcast(U32)
            nc.vector.tensor_copy(
                picked[q // 2][:, q % 2, V * first : V * last],
                window.indirect(picks[:, LIST_COLS * first : LIST_COLS * last]),
            )

        def weave(g, d, into, on_vector):
            src = picked[g][:, :, V * d : V * (d + 1)]
            if on_vector:
                nc.vector.tensor_copy(
                    into.bitcast(I32).rearrange("p (v u) -> p v u", u=2),
                    src.bitcast(I32).rearrange("p u v -> p v u"),
                )
            else:
                nc.scalar.copy(
                    into.bitcast(U32).rearrange("p (v u) -> p v u", u=2),
                    src.rearrange("p u v -> p v u"),
                )

        def quantise(woven, operands, tag=None):
            width = V * len(operands)
            name = "_".join(f"{g}{d}" for g, d in operands)
            words = keep.tile([P, width], U32, name=f"codes{name}", tag=tag or f"codes{name}", align_bytes=64)
            planes = keep.tile([P, width], U8, name=f"scale{name}", align_bytes=64)
            nc.vector.quantize_mx(out=words[:].bitcast(FP8X4), scales=planes[:], in_=woven[:])
            for i, operand in enumerate(operands):
                codes[operand] = words[:, V * i : V * (i + 1)]
                scale[operand] = planes[:, V * i : V * (i + 1)]

        def multiply(g, d):
            nc.tensor.matmul_mx(
                out=acc[d][:],
                lhsT=w_codes[d][:, g, :].bitcast(FP4X4),
                lhsT_scale=w_scales[:, PASSES * d + g, :],
                rhs=codes[g, d].bitcast(FP8X4),
                rhs_scale=scale[g, d],
                start=(g == 0),
                stop=(g == PASSES - 1),
            )

        woven = {
            (g, d): keep.tile([P, 4 * V], BF16, name=f"woven{g}_{d}", tag=f"woven{g}_{d}", align_bytes=64)
            for g in range(PASSES)
            for d in range(TAPS)
            if (g, d) != (0, 2)
        }
        cast(0)
        gather(0, 0, TAPS)
        cast(1)
        gather(1, 0, 1)
        gather(1, 1, TAPS)
        cast(2)
        for d in range(2):
            weave(0, d, woven[0, d][:], True)
        for d in range(2):
            quantise(woven[0, d], [(0, d)])
            multiply(0, d)
        gather(2, 0, TAPS)
        cast(3)
        woven[0, 2] = keep.tile([P, 4 * V], BF16, name="woven0_2", tag="raw3_3", align_bytes=64)
        weave(0, 2, woven[0, 2][:], False)
        for d in range(TAPS):
            gather(3, d, d + 1)
        for d in range(TAPS):
            weave(1, d, woven[1, d][:], False)
        for d in range(2):
            quantise(woven[1, d], [(1, d)])
            multiply(1, d)
        quantise(woven[0, 2], [(0, 2)], "woven1_1")
        quantise(woven[1, 2], [(1, 2)])
        multiply(0, 2)
        multiply(1, 2)

        for d in range(TAPS):
            y = keep.tile([P, V], F32, name=f"y{d}")
            nc.scalar.copy(y[:], acc[d][:])
            nc.vector.tensor_copy(spread[d][:].indirect(places[d][:]), y[:])

        halves = U // BANK
        blocks = BANK // P
        turned = [psum.tile([P, BANK], F32, name=f"turned{h}") for h in range(halves)]
        for d in range(2):
            for h in range(halves):
                for b in range(blocks):
                    nc.tensor.matmul(
                        turned[h][:, P * b : P * (b + 1)],
                        spread[d][:, BANK * h + P * b : BANK * h + P * (b + 1)],
                        ident[:],
                        start=(d == 0 and b == 0),
                        stop=(d == 1 and b == blocks - 1),
                        is_transpose=True,
                    )
        two_taps = [psum.tile([P, BANK], F32, name=f"two_taps{h}") for h in range(halves)]
        for h in range(halves):
            held = keep.tile([P, BANK], F32, name=f"held{h}")
            nc.scalar.copy(held[:], turned[h][:])
            for b in range(blocks):
                nc.tensor.transpose(two_taps[h][:, P * b : P * (b + 1)], held[:, P * b : P * (b + 1)], ident[:])

        for c0 in range(0, U, OUT_CHUNK):
            h, at = divmod(c0, BANK)
            total = keep.tile([P, OUT_CHUNK], F32, name=f"total{c0}")
            result = keep.tile([P, OUT_CHUNK], F32, name=f"result{c0}")
            nc.vector.tensor_tensor(total[:], spread[2][:, c0 : c0 + OUT_CHUNK], two_taps[h][:, at : at + OUT_CHUNK], ADD)
            nc.scalar.activation(result[:], total[:], RELU)
            nc.sync.dma_start(out[:, c0 : c0 + OUT_CHUNK], result[:])
